import numpy as np
import ml_dtypes


def mxq(x, axis, fmt="e4m3"):
    dtype, down = {"e4m3": (ml_dtypes.float8_e4m3fn, 7), "e5m2": (ml_dtypes.float8_e5m2, 14)}[fmt]
    v = np.moveaxis(np.asarray(x, np.float32).astype(ml_dtypes.bfloat16).astype(np.float64), axis, -1)
    blocks = v.reshape(v.shape[:-1] + (-1, 32))
    amax = np.abs(blocks).max(-1, keepdims=True)
    byte = np.maximum(np.where(amax > 0, np.frexp(amax)[1] - 1 + 127, 0) - down, 1)
    scale = np.exp2(byte - 127.0)
    codes = (blocks / scale).astype(np.float32).astype(dtype).astype(np.float64)
    return np.moveaxis((codes * scale).reshape(v.shape), -1, axis)


WIDE = False


def mx_kscale(k):
    if not WIDE:
        return np.ones(k)
    levels = np.array([10, -10, 5, -5, 0])
    if k % 512:
        return np.exp2(np.random.permutation(np.resize(levels, k // 32))).repeat(32)
    a = np.empty((k // 512, 16))
    for p in range(k // 512):
        a[p, :8] = np.random.permutation(np.resize(levels, 8))
        for g in range(8):
            far = levels[np.abs(levels - a[p, g]) >= 10]
            a[p, g + 8] = far[np.random.randint(len(far))]
    return np.exp2(a.ravel()).repeat(32)


def f64(x):
    return np.asarray(x).astype(np.float64)


def striped(idx):
    return np.tile(idx.reshape(-1, 16).T, (8, 1)).astype(np.uint16)


def unstriped(offs):
    return offs[:16].T.reshape(-1).astype(np.int64)


K, T, S, D, V, H, N = 512, 1024, 512, 4, 256, 512, 256
P = 2 ** 7


def setup_inputs():
    n = np.random.standard_normal
    s = mx_kscale(K)[:, None]
    u = mx_kscale(H)
    return {
        "xT": (n((K, T)) * s).astype(np.float32),
        "w1": (n((K, H)) / np.sqrt(K) / s * u).astype(np.float32),
        "w2": (n((H, N)) / np.sqrt(H) / u[:, None]).astype(np.float32),
        "gate": (np.tile(np.random.uniform(0.2, 1.0, (D, 1, V)) / np.sqrt(D), (1, P, 1))).astype(np.float32),
        "offs": striped(np.random.permutation(T)[:S]),
        "cen": striped(np.random.permutation(S)[:V]),
        "pos1": striped(np.random.permutation(S)[:V]),
        "pos2": striped(np.random.permutation(S)[:V]),
        "pos3": striped(np.random.permutation(S)[:V]),
        "pos4": striped(np.random.permutation(S)[:V]),
    }


def reference(xT, w1, w2, gate, offs, cen, pos1, pos2, pos3, pos4):
    xq = mxq(f64(xT)[:, unstriped(offs)], 0, "e4m3")
    h = mxq(f64(w1), 0, "e4m3").T @ xq
    z = h[:, unstriped(cen)] - (h[:, unstriped(pos1)] * f64(gate)[0, :1] + h[:, unstriped(pos2)] * f64(gate)[1, :1] + h[:, unstriped(pos3)] * f64(gate)[2, :1] + h[:, unstriped(pos4)] * f64(gate)[3, :1])
    return mxq(f64(w2), 0, "e4m3").T @ mxq(z, 0, "e4m3")

@@ -1,0 +1,205 @@
+from contextlib import ExitStack
+
+import concourse.mybir as mybir
+from concourse.masks import make_identity
+
+K, T, S, D, V, H, N = 512, 1024, 512, 4, 256, 512, 256
+FLOPS = 2 * K * H * S + 2 * H * N * V
+
+F32 = mybir.dt.float32
+BF16 = mybir.dt.bfloat16
+U32 = mybir.dt.uint32
+U16 = mybir.dt.uint16
+U8 = mybir.dt.uint8
+FP8X4 = mybir.dt.float8_e4m3fn_x4
+MULT = mybir.AluOpType.mult
+COPY = mybir.ActivationFunctionType.Copy
+
+P = 128
+
+
+def tile_picked_lapl_none_e_kernel(
+    tc, xT, w1, w2, gate, offs, cen, pos1, pos2, pos3, pos4, out
+):
+    nc = tc.nc
+    with ExitStack() as ctx:
+        keep = ctx.enter_context(tc.tile_pool(name="keep", bufs=1))
+        terms = ctx.enter_context(tc.tile_pool(name="terms", bufs=10))
+        acc_pool = ctx.enter_context(tc.psum_pool(name="acc", bufs=2))
+        zt_pool = ctx.enter_context(tc.psum_pool(name="zt", bufs=4))
+        back_pool = ctx.enter_context(tc.psum_pool(name="back", bufs=1))
+
+        x_rows = xT.rearrange("(p j) t -> p j t", j=4)
+        x_plane = [keep.tile([P, T], F32, name=f"x_plane{j}") for j in range(4)]
+        offs_sb = keep.tile([P, S // 16], U16, name="offs_sb")
+        nc.sync.dma_start(out=x_plane[0][:], in_=x_rows[:, 0, :])
+        nc.sync.dma_start(offs_sb[:], offs)
+        for j in range(1, 4):
+            nc.sync.dma_start(out=x_plane[j][:], in_=x_rows[:, j, :])
+        w1_rows = w1.rearrange("(p j) c -> p j c", j=4)
+        w1_half = [keep.tile([P, 4, H // 2], F32, name=f"w1_half{a}") for a in range(2)]
+        for a in range(2):
+            nc.sync.dma_start(out=w1_half[a][:], in_=w1_rows[:, :, a * 256 : (a + 1) * 256])
+        gate_rows = keep.tile([P, V], F32, name="gate_rows")
+        nc.gpsimd.memset(gate_rows[:], 0.0)
+        nc.scalar.dma_start(out=gate_rows[0:D, :], in_=gate[:, 0, :])
+        lists = []
+        for name, src in (("cen", cen), ("pos1", pos1), ("pos2", pos2), ("pos3", pos3), ("pos4", pos4)):
+            t_list = keep.tile([P, V // 16], U16, name=f"{name}_sb")
+            nc.sync.dma_start(t_list[:], src)
+            lists.append(t_list)
+        w2_raw = keep.tile([P, 4, N], F32, name="w2_raw")
+        nc.sync.dma_start(out=w2_raw[:], in_=w2.rearrange("(p j) m -> p j m", j=4))
+
+        ident = keep.tile([P, P], F32, name="ident")
+        make_identity(nc, ident[:])
+
+        gate_t = acc_pool.tile([P, 2, P], F32, name="gate_t", tag="acc")
+        for b in range(2):
+            nc.tensor.transpose(gate_t[:, b, :], gate_rows[:, b * P : (b + 1) * P], ident[:])
+        gate_cols = keep.tile([P, 2, D], F32, name="gate_cols")
+        nc.scalar.activation(out=gate_cols[:], in_=gate_t[:, :, 0:D], func=COPY, scale=-1.0)
+        neg_gate = [keep.tile([P, 2, V], F32, name=f"neg_gate{c}") for c in range(2)]
+        for c in range(2):
+            spread = acc_pool.tile([P, 2, V], F32, name="spread", tag="acc")
+            for dd in range(2):
+                d = 2 * c + dd
+                for b in range(2):
+                    nc.tensor.transpose(
+                        spread[:, dd, b * P : (b + 1) * P],
+                        gate_cols[:, b, d : d + 1].to_broadcast([P, P]),
+                        ident[:],
+                    )
+            nc.scalar.copy(out=neg_gate[c][:], in_=spread[:])
+
+        picked = [keep.tile([P, 2, S], F32, name=f"picked{u}") for u in range(2)]
+        x_grouped = keep.tile([P, S * 4], BF16, name="x_grouped", align_bytes=64)
+        xg = x_grouped[:].rearrange("p (n u e) -> p u n e", u=2, e=2)
+        for u in range(2):
+            for e in range(2):
+                nc.vector.tensor_copy(picked[u][:, e, :], x_plane[2 * u + e][:].indirect(offs_sb[:]))
+            if u == 0:
+                nc.scalar.copy(out=xg[:, 0], in_=picked[0][:].rearrange("p e n -> p n e"))
+            else:
+                nc.vector.tensor_copy(out=xg[:, 1], in_=picked[1][:].rearrange("p e n -> p n e"))
+
+        tiles = [(0, 0), (0, 1), (1, 0), (1, 1)]
+        w_codes, w_scales = [], []
+
+        def quantize_w1(t):
+            a, u = tiles[t]
+            grouped = keep.tile([P, 512], BF16, name=f"w1_grouped{t}", align_bytes=64)
+            nc.scalar.copy(
+                out=grouped[:].rearrange("p (m e j) -> p m j e", e=2, j=4),
+                in_=w1_half[a][:].rearrange("p j (m u e) -> p u m j e", u=2, e=2)[:, u],
+            )
+            codes = keep.tile([P, P], U32, name=f"w1_codes{t}", align_bytes=64)
+            scales = keep.tile([P, P], U8, name=f"w1_scales{t}", align_bytes=64)
+            nc.vector.quantize_mx(out=codes[:].bitcast(FP8X4), scales=scales[:], in_=grouped[:])
+            w_codes.append(codes)
+            w_scales.append(scales)
+
+        quantize_w1(0)
+        x_codes = keep.tile([P, S], U32, name="x_codes", align_bytes=64)
+        x_scales = keep.tile([P, S], U8, name="x_scales", align_bytes=64)
+        for b in range(2):
+            nc.vector.quantize_mx(
+                out=x_codes[:, b * 256 : (b + 1) * 256].bitcast(FP8X4),
+                scales=x_scales[:, b * 256 : (b + 1) * 256],
+                in_=x_grouped[:, b * 1024 : (b + 1) * 1024],
+            )
+
+        h = [keep.tile([P, S], F32, name=f"h{t}") for t in range(4)]
+
+        def first_product(t, cols, copy):
+            width = cols.stop - cols.start
+            acc = acc_pool.tile([P, width], F32, name="h_acc", tag="acc")
+            nc.tensor.matmul_mx(
+                out=acc[:],
+                lhsT=w_codes[t][:].bitcast(FP8X4),
+                lhsT_scale=w_scales[t][:],
+                rhs=x_codes[:, cols].bitcast(FP8X4),
+                rhs_scale=x_scales[:, cols],
+                start=True,
+                stop=True,
+            )
+            copy(out=h[t][:, cols], in_=acc[:])
+
+        first_product(0, slice(0, 256), nc.scalar.copy)
+        first_product(0, slice(256, 512), nc.vector.tensor_copy)
+        for t in range(1, 4):
+            quantize_w1(t)
+            first_product(t, slice(0, S), nc.scalar.copy)
+
+        w2_grouped = keep.tile([P, N * 4], BF16, name="w2_grouped", align_bytes=64)
+        nc.scalar.copy(
+            out=w2_grouped[:].rearrange("p (c i j) -> p c j i", i=4, j=4),
+            in_=w2_raw[:].rearrange("p j (c i) -> p c j i", i=4),
+        )
+        w2_codes = keep.tile([P, N], U32, name="w2_codes", align_bytes=64)
+        w2_scales = keep.tile([P, N], U8, name="w2_scales", align_bytes=64)
+
+        z_pairs = [[keep.tile([P, 2 * P], BF16, name=f"z_pairs{b}{u}") for u in range(2)] for b in range(2)]
+        back = [back_pool.tile([P, 2, P], F32, name=f"back{b}") for b in range(2)]
+        out_view = out.rearrange("(m p) v -> p m v", p=P)
+
+        def laplacian(t, halves):
+            a, u = tiles[t]
+            cols = slice(halves[0] * P, (halves[-1] + 1) * P)
+            list_cols = slice(cols.start // 16, cols.stop // 16)
+            width = cols.stop - cols.start
+            sums = [zt_pool.tile([P, P], F32, name="z_t", tag="zt") for b in halves]
+            for r in range(D + 1):
+                term = terms.tile([P, V], F32, name="term")
+                window = h[t][:].indirect(lists[r][:, list_cols])
+                if r == 0:
+                    nc.vector.tensor_copy(term[:, 0:width], window)
+                else:
+                    d = r - 1
+                    nc.vector.tensor_tensor(term[:, 0:width], window, neg_gate[d // 2][:, d % 2, cols], MULT)
+                for n, b in enumerate(halves):
+                    nc.tensor.matmul(
+                        sums[n][:],
+                        lhsT=term[:, n * P : (n + 1) * P],
+                        rhs=ident[:],
+                        is_transpose=True,
+                        start=(r == 0),
+                        stop=(r == D),
+                    )
+            for n, b in enumerate(halves):
+                nc.scalar.copy(out=z_pairs[b][u][:, a * P : (a + 1) * P], in_=sums[n][:])
+                if a == 1:
+                    nc.tensor.transpose(back[b][:, u, :], z_pairs[b][u][:].bitcast(F32), ident[:])
+
+        def finish(b):
+            grouped = keep.tile([P, P * 4], BF16, name=f"z_grouped{b}", align_bytes=64)
+            nc.scalar.copy(
+                out=grouped[:].bitcast(F32).rearrange("p (v u) -> p v u", u=2),
+                in_=back[b][:].rearrange("p u v -> p v u"),
+            )
+            codes = keep.tile([P, P], U32, name=f"z_codes{b}", align_bytes=64)
+            scales = keep.tile([P, P], U8, name=f"z_scales{b}", align_bytes=64)
+            nc.vector.quantize_mx(out=codes[:].bitcast(FP8X4), scales=scales[:], in_=grouped[:])
+            acc = acc_pool.tile([P, 2, P], F32, name="out_acc", tag="acc")
+            for m in range(2):
+                nc.tensor.matmul_mx(
+                    out=acc[:, m, :],
+                    lhsT=w2_codes[:, m * P : (m + 1) * P].bitcast(FP8X4),
+                    lhsT_scale=w2_scales[:, m * P : (m + 1) * P],
+                    rhs=codes[:].bitcast(FP8X4),
+                    rhs_scale=scales[:],
+                    start=True,
+                    stop=True,
+                )
+            result = keep.tile([P, 2, P], F32, name=f"result{b}")
+            nc.scalar.copy(out=result[:], in_=acc[:])
+            nc.sync.dma_start(out=out_view[:, :, b * P : (b + 1) * P], in_=result[:])
+
+        laplacian(0, [0, 1])
+        laplacian(1, [0, 1])
+        nc.vector.quantize_mx(out=w2_codes[:].bitcast(FP8X4), scales=w2_scales[:], in_=w2_grouped[:])
+        laplacian(2, [0, 1])
+        laplacian(3, [0])
+        laplacian(3, [1])
+        finish(0)
+        finish(1)

@@ -13,6 +13,7 @@ U16 = mybir.dt.uint16
 U8 = mybir.dt.uint8
 FP8X4 = mybir.dt.float8_e4m3fn_x4
 MULT = mybir.AluOpType.mult
+ADD = mybir.AluOpType.add
 COPY = mybir.ActivationFunctionType.Copy
 
 P = 128
@@ -24,182 +25,191 @@ def tile_picked_lapl_none_e_kernel(
     nc = tc.nc
     with ExitStack() as ctx:
         keep = ctx.enter_context(tc.tile_pool(name="keep", bufs=1))
-        terms = ctx.enter_context(tc.tile_pool(name="terms", bufs=10))
-        acc_pool = ctx.enter_context(tc.psum_pool(name="acc", bufs=2))
-        zt_pool = ctx.enter_context(tc.psum_pool(name="zt", bufs=4))
-        back_pool = ctx.enter_context(tc.psum_pool(name="back", bufs=1))
+        psum = ctx.enter_context(tc.psum_pool(name="psum", bufs=1))
 
+        def bank(k, shape, name):
+            return psum.tile(shape, F32, name=name, tag=f"bank{k}")
+
+        def quantize(codes, scales, grouped):
+            nc.vector.quantize_mx(out=codes.bitcast(FP8X4), scales=scales, in_=grouped)
+
+        def product(acc, w_codes, w_scales, a_codes, a_scales):
+            nc.tensor.matmul_mx(
+                out=acc,
+                lhsT=w_codes.bitcast(FP8X4),
+                lhsT_scale=w_scales,
+                rhs=a_codes.bitcast(FP8X4),
+                rhs_scale=a_scales,
+                start=True,
+                stop=True,
+            )
+
+        offs_sb = keep.tile([P, S // 16], U16, name="offs_sb")
+        nc.sync.dma_start(offs_sb[:], offs)
         x_rows = xT.rearrange("(p j) t -> p j t", j=4)
         x_plane = [keep.tile([P, T], F32, name=f"x_plane{j}") for j in range(4)]
-        offs_sb = keep.tile([P, S // 16], U16, name="offs_sb")
         nc.sync.dma_start(out=x_plane[0][:], in_=x_rows[:, 0, :])
-        nc.sync.dma_start(offs_sb[:], offs)
+        gate_runs = keep.tile([P, 8], F32, name="gate_runs")
+        nc.sync.dma_start(out=gate_runs[:], in_=gate.rearrange("d p (c i) -> (d p c) i", i=8)[0 : D * P * V // 8 : 129, :])
         for j in range(1, 4):
             nc.sync.dma_start(out=x_plane[j][:], in_=x_rows[:, j, :])
         w1_rows = w1.rearrange("(p j) c -> p j c", j=4)
         w1_half = [keep.tile([P, 4, H // 2], F32, name=f"w1_half{a}") for a in range(2)]
         for a in range(2):
             nc.sync.dma_start(out=w1_half[a][:], in_=w1_rows[:, :, a * 256 : (a + 1) * 256])
-        gate_rows = keep.tile([P, V], F32, name="gate_rows")
-        nc.gpsimd.memset(gate_rows[:], 0.0)
-        nc.scalar.dma_start(out=gate_rows[0:D, :], in_=gate[:, 0, :])
         lists = []
-        for name, src in (("cen", cen), ("pos1", pos1), ("pos2", pos2), ("pos3", pos3), ("pos4", pos4)):
-            t_list = keep.tile([P, V // 16], U16, name=f"{name}_sb")
-            nc.sync.dma_start(t_list[:], src)
-            lists.append(t_list)
+        for name, src in (("pos1", pos1), ("pos2", pos2), ("pos3", pos3), ("pos4", pos4), ("cen", cen)):
+            list_sb = keep.tile([P, V // 16], U16, name=f"{name}_sb")
+            nc.sync.dma_start(list_sb[:], src)
+            lists.append(list_sb)
+        cen_sb = lists[D]
         w2_raw = keep.tile([P, 4, N], F32, name="w2_raw")
         nc.sync.dma_start(out=w2_raw[:], in_=w2.rearrange("(p j) m -> p j m", j=4))
 
         ident = keep.tile([P, P], F32, name="ident")
         make_identity(nc, ident[:])
 
-        gate_t = acc_pool.tile([P, 2, P], F32, name="gate_t", tag="acc")
-        for b in range(2):
-            nc.tensor.transpose(gate_t[:, b, :], gate_rows[:, b * P : (b + 1) * P], ident[:])
-        gate_cols = keep.tile([P, 2, D], F32, name="gate_cols")
-        nc.scalar.activation(out=gate_cols[:], in_=gate_t[:, :, 0:D], func=COPY, scale=-1.0)
-        neg_gate = [keep.tile([P, 2, V], F32, name=f"neg_gate{c}") for c in range(2)]
+        neg_gate = keep.tile([P, D * V], F32, name="neg_gate")
         for c in range(2):
-            spread = acc_pool.tile([P, 2, V], F32, name="spread", tag="acc")
-            for dd in range(2):
-                d = 2 * c + dd
-                for b in range(2):
-                    nc.tensor.transpose(
-                        spread[:, dd, b * P : (b + 1) * P],
-                        gate_cols[:, b, d : d + 1].to_broadcast([P, P]),
-                        ident[:],
-                    )
-            nc.scalar.copy(out=neg_gate[c][:], in_=spread[:])
-
-        picked = [keep.tile([P, 2, S], F32, name=f"picked{u}") for u in range(2)]
-        x_grouped = keep.tile([P, S * 4], BF16, name="x_grouped", align_bytes=64)
-        xg = x_grouped[:].rearrange("p (n u e) -> p u n e", u=2, e=2)
-        for u in range(2):
-            for e in range(2):
-                nc.vector.tensor_copy(picked[u][:, e, :], x_plane[2 * u + e][:].indirect(offs_sb[:]))
-            if u == 0:
-                nc.scalar.copy(out=xg[:, 0], in_=picked[0][:].rearrange("p e n -> p n e"))
-            else:
-                nc.vector.tensor_copy(out=xg[:, 1], in_=picked[1][:].rearrange("p e n -> p n e"))
-
-        tiles = [(0, 0), (0, 1), (1, 0), (1, 1)]
-        w_codes, w_scales = [], []
-
-        def quantize_w1(t):
-            a, u = tiles[t]
-            grouped = keep.tile([P, 512], BF16, name=f"w1_grouped{t}", align_bytes=64)
-            nc.scalar.copy(
-                out=grouped[:].rearrange("p (m e j) -> p m j e", e=2, j=4),
-                in_=w1_half[a][:].rearrange("p j (m u e) -> p u m j e", u=2, e=2)[:, u],
+            spread = bank(c, [P, 4, P], "spread")
+            for i in range(4):
+                nc.tensor.transpose(
+                    spread[:, i, :], gate_runs[:, 4 * c + i : 4 * c + i + 1].to_broadcast([P, P]), ident[:]
+                )
+            nc.scalar.activation(
+                out=neg_gate[:].rearrange("p (q c i) -> p c q i", c=2, i=4)[:, c],
+                in_=spread[:].rearrange("p i q -> p q i"),
+                func=COPY,
+                scale=-1.0,
             )
-            codes = keep.tile([P, P], U32, name=f"w1_codes{t}", align_bytes=64)
-            scales = keep.tile([P, P], U8, name=f"w1_scales{t}", align_bytes=64)
-            nc.vector.quantize_mx(out=codes[:].bitcast(FP8X4), scales=scales[:], in_=grouped[:])
-            w_codes.append(codes)
-            w_scales.append(scales)
 
-        quantize_w1(0)
+        node_halves = [slice(0, S // 2), slice(S // 2, S)]
+        x_grouped = [keep.tile([P, 2 * S], BF16, name=f"x_grouped{b}", align_bytes=64) for b in range(2)]
+        for u, weave in enumerate((nc.scalar.copy, nc.vector.tensor_copy)):
+            picked = keep.tile([P, 2, S], F32, name=f"picked{u}")
+            for e in range(2):
+                nc.vector.tensor_copy(picked[:, e, :], x_plane[2 * u + e][:].indirect(offs_sb[:]))
+            for b in range(2):
+                weave(
+                    out=x_grouped[b][:].rearrange("p (n u e) -> p u n e", u=2, e=2)[:, u],
+                    in_=picked[:, :, node_halves[b]].rearrange("p e n -> p n e"),
+                )
+
+        w1_grouped = []
+        for u in range(2):
+            grouped = keep.tile([P, 2 * K], BF16, name=f"w1_grouped{u}", tag=f"w1_slot{u}", align_bytes=64)
+            for a in range(2):
+                nc.scalar.copy(
+                    out=grouped[:].rearrange("p (e a m j) -> p a m j e", e=2, a=2, j=4)[:, a],
+                    in_=w1_half[a][:].rearrange("p j (m u e) -> p u m j e", u=2, e=2)[:, u],
+                )
+            w1_grouped.append(grouped)
+
+        w1_scales = keep.tile([P, H], U8, name="w1_scales", align_bytes=64)
+        first_codes = keep.tile([P, P], U32, name="first_codes", tag="w1_codes", align_bytes=64)
+        quantize(first_codes[:], w1_scales[:, 0:P], w1_grouped[0][:, 0:K])
         x_codes = keep.tile([P, S], U32, name="x_codes", align_bytes=64)
         x_scales = keep.tile([P, S], U8, name="x_scales", align_bytes=64)
         for b in range(2):
-            nc.vector.quantize_mx(
-                out=x_codes[:, b * 256 : (b + 1) * 256].bitcast(FP8X4),
-                scales=x_scales[:, b * 256 : (b + 1) * 256],
-                in_=x_grouped[:, b * 1024 : (b + 1) * 1024],
-            )
+            quantize(x_codes[:, node_halves[b]], x_scales[:, node_halves[b]], x_grouped[b][:])
 
         h = [keep.tile([P, S], F32, name=f"h{t}") for t in range(4)]
+        for b, copy in enumerate((nc.vector.tensor_copy, nc.scalar.copy)):
+            cols = node_halves[b]
+            acc = bank(4 + b, [P, S // 2], "h_acc")
+            product(acc[:], first_codes[:], w1_scales[:, 0:P], x_codes[:, cols], x_scales[:, cols])
+            copy(out=h[0][:, cols], in_=acc[:])
 
-        def first_product(t, cols, copy):
-            width = cols.stop - cols.start
-            acc = acc_pool.tile([P, width], F32, name="h_acc", tag="acc")
-            nc.tensor.matmul_mx(
-                out=acc[:],
-                lhsT=w_codes[t][:].bitcast(FP8X4),
-                lhsT_scale=w_scales[t][:],
-                rhs=x_codes[:, cols].bitcast(FP8X4),
-                rhs_scale=x_scales[:, cols],
-                start=True,
-                stop=True,
+        later_codes = keep.tile([P, 3 * P], U32, name="later_codes", tag="w1_codes", align_bytes=64)
+        quantize(later_codes[:, 0:P], w1_scales[:, P : 2 * P], w1_grouped[0][:, K : 2 * K])
+        quantize(later_codes[:, P : 3 * P], w1_scales[:, 2 * P : 4 * P], w1_grouped[1][:])
+        for t, k in ((1, 6), (2, 7), (3, 4)):
+            acc = bank(k, [P, S], "h_acc")
+            product(
+                acc[:], later_codes[:, (t - 1) * P : t * P], w1_scales[:, t * P : (t + 1) * P], x_codes[:], x_scales[:]
             )
-            copy(out=h[t][:, cols], in_=acc[:])
+            nc.scalar.copy(out=h[t][:], in_=acc[:])
 
-        first_product(0, slice(0, 256), nc.scalar.copy)
-        first_product(0, slice(256, 512), nc.vector.tensor_copy)
-        for t in range(1, 4):
-            quantize_w1(t)
-            first_product(t, slice(0, S), nc.scalar.copy)
+        target_halves = [slice(0, P), slice(P, V)]
+        slots = {(0, 1): "w1_slot0", (0, 2): "w1_slot1", (0, 3): "w2_slot"}
 
-        w2_grouped = keep.tile([P, N * 4], BF16, name="w2_grouped", align_bytes=64)
+        def neighbour_sum(t, back_banks):
+            sums = [bank(2 * (t % 2) + b, [P, P], "turned_sum") for b in range(2)]
+            for d in range(D):
+                term = keep.tile([P, V], F32, name="term", tag=slots.get((t, d), f"term{t}{d}"), align_bytes=64)
+                nc.vector.tensor_tensor(term[:], h[t][:].indirect(lists[d][:]), neg_gate[:, d * V : (d + 1) * V], MULT)
+                for b in range(2):
+                    nc.tensor.matmul(
+                        sums[b][:],
+                        lhsT=term[:, target_halves[b]],
+                        rhs=ident[:],
+                        is_transpose=True,
+                        start=(d == 0),
+                        stop=(d == D - 1),
+                    )
+            partial = keep.tile([P, V], F32, name=f"partial{t}")
+            width = V // len(back_banks)
+            back = [bank(k, [P, width], "back") for k in back_banks]
+            for b in range(2):
+                turned = keep.tile([P, P], F32, name="turned", tag=f"turned{t}{b}", align_bytes=64)
+                nc.scalar.copy(out=turned[:], in_=sums[b][:])
+                n, first = divmod(b * P, width)
+                nc.tensor.transpose(back[n][:, first : first + P], turned[:], ident[:])
+            for n in range(len(back_banks)):
+                nc.scalar.copy(out=partial[:, n * width : (n + 1) * width], in_=back[n][:])
+            return partial
+
+        partials = [neighbour_sum(0, [5])]
+        w2_grouped = keep.tile([P, N * 4], BF16, name="w2_grouped", tag="w2_slot", align_bytes=64)
         nc.scalar.copy(
             out=w2_grouped[:].rearrange("p (c i j) -> p c j i", i=4, j=4),
             in_=w2_raw[:].rearrange("p j (c i) -> p c j i", i=4),
         )
+        partials.append(neighbour_sum(1, [6]))
+        partials.append(neighbour_sum(2, [7]))
+        partials.append(neighbour_sum(3, [4, 5]))
+
         w2_codes = keep.tile([P, N], U32, name="w2_codes", align_bytes=64)
         w2_scales = keep.tile([P, N], U8, name="w2_scales", align_bytes=64)
+        quantize(w2_codes[:], w2_scales[:], w2_grouped[:])
 
-        z_pairs = [[keep.tile([P, 2 * P], BF16, name=f"z_pairs{b}{u}") for u in range(2)] for b in range(2)]
-        back = [back_pool.tile([P, 2, P], F32, name=f"back{b}") for b in range(2)]
-        out_view = out.rearrange("(m p) v -> p m v", p=P)
-
-        def laplacian(t, halves):
-            a, u = tiles[t]
-            cols = slice(halves[0] * P, (halves[-1] + 1) * P)
-            list_cols = slice(cols.start // 16, cols.stop // 16)
-            width = cols.stop - cols.start
-            sums = [zt_pool.tile([P, P], F32, name="z_t", tag="zt") for b in halves]
-            for r in range(D + 1):
-                term = terms.tile([P, V], F32, name="term")
-                window = h[t][:].indirect(lists[r][:, list_cols])
-                if r == 0:
-                    nc.vector.tensor_copy(term[:, 0:width], window)
-                else:
-                    d = r - 1
-                    nc.vector.tensor_tensor(term[:, 0:width], window, neg_gate[d // 2][:, d % 2, cols], MULT)
-                for n, b in enumerate(halves):
-                    nc.tensor.matmul(
-                        sums[n][:],
-                        lhsT=term[:, n * P : (n + 1) * P],
-                        rhs=ident[:],
-                        is_transpose=True,
-                        start=(r == 0),
-                        stop=(r == D),
-                    )
-            for n, b in enumerate(halves):
-                nc.scalar.copy(out=z_pairs[b][u][:, a * P : (a + 1) * P], in_=sums[n][:])
-                if a == 1:
-                    nc.tensor.transpose(back[b][:, u, :], z_pairs[b][u][:].bitcast(F32), ident[:])
-
-        def finish(b):
-            grouped = keep.tile([P, P * 4], BF16, name=f"z_grouped{b}", align_bytes=64)
-            nc.scalar.copy(
-                out=grouped[:].bitcast(F32).rearrange("p (v u) -> p v u", u=2),
-                in_=back[b][:].rearrange("p u v -> p v u"),
-            )
-            codes = keep.tile([P, P], U32, name=f"z_codes{b}", align_bytes=64)
-            scales = keep.tile([P, P], U8, name=f"z_scales{b}", align_bytes=64)
-            nc.vector.quantize_mx(out=codes[:].bitcast(FP8X4), scales=scales[:], in_=grouped[:])
-            acc = acc_pool.tile([P, 2, P], F32, name="out_acc", tag="acc")
-            for m in range(2):
-                nc.tensor.matmul_mx(
-                    out=acc[:, m, :],
-                    lhsT=w2_codes[:, m * P : (m + 1) * P].bitcast(FP8X4),
-                    lhsT_scale=w2_scales[:, m * P : (m + 1) * P],
-                    rhs=codes[:].bitcast(FP8X4),
-                    rhs_scale=scales[:],
-                    start=True,
-                    stop=True,
+        z_grouped = [
+            keep.tile([P, 4 * P], BF16, name=f"z_grouped{b}", tag=f"turned3{b}", align_bytes=64) for b in range(2)
+        ]
+        z_slots = [g[:].rearrange("p (v u e) -> p u v e", u=2, e=2) for g in z_grouped]
+        z01 = keep.tile([P, 2, V], F32, name="z01")
+        for t in range(2):
+            nc.vector.tensor_tensor(z01[:, t, :], h[t][:].indirect(cen_sb[:]), partials[t][:], ADD)
+        for b in range(2):
+            nc.scalar.copy(out=z_slots[b][:, 0], in_=z01[:, :, target_halves[b]].rearrange("p e v -> p v e"))
+        z23 = [keep.tile([P, 2, P], F32, name=f"z23_{b}") for b in range(2)]
+        for t in range(2, 4):
+            for b in range(2):
+                nc.vector.tensor_tensor(
+                    z23[b][:, t - 2, :],
+                    h[t][:].indirect(cen_sb[:, b * 8 : (b + 1) * 8]),
+                    partials[t][:, target_halves[b]],
+                    ADD,
                 )
-            result = keep.tile([P, 2, P], F32, name=f"result{b}")
-            nc.scalar.copy(out=result[:], in_=acc[:])
-            nc.sync.dma_start(out=out_view[:, :, b * P : (b + 1) * P], in_=result[:])
+        for b in range(2):
+            nc.vector.tensor_copy(out=z_slots[b][:, 1], in_=z23[b][:].rearrange("p e v -> p v e"))
+        z_codes = [keep.tile([P, P], U32, name=f"z_codes{b}", align_bytes=64) for b in range(2)]
+        z_scales = [keep.tile([P, P], U8, name=f"z_scales{b}", align_bytes=64) for b in range(2)]
+        for b in range(2):
+            quantize(z_codes[b][:], z_scales[b][:], z_grouped[b][:])
 
-        laplacian(0, [0, 1])
-        laplacian(1, [0, 1])
-        nc.vector.quantize_mx(out=w2_codes[:].bitcast(FP8X4), scales=w2_scales[:], in_=w2_grouped[:])
-        laplacian(2, [0, 1])
-        laplacian(3, [0])
-        laplacian(3, [1])
-        finish(0)
-        finish(1)
+        out_view = out.rearrange("(m p) v -> p m v", p=P)
+        acc = bank(0, [P, 2, P], "out_acc")
+        for m in range(2):
+            rows = slice(m * P, (m + 1) * P)
+            product(acc[:, m, :], w2_codes[:, rows], w2_scales[:, rows], z_codes[0][:], z_scales[0][:])
+        result = keep.tile([P, 2, P], F32, name="result0")
+        nc.scalar.copy(out=result[:], in_=acc[:])
+        nc.sync.dma_start(out=out_view[:, :, target_halves[0]], in_=result[:])
+        for m, copy, queue in ((0, nc.vector.tensor_copy, nc.sync), (1, nc.scalar.copy, nc.scalar)):
+            rows = slice(m * P, (m + 1) * P)
+            acc_m = bank(1 + m, [P, P], "out_m")
+            product(acc_m[:], w2_codes[:, rows], w2_scales[:, rows], z_codes[1][:], z_scales[1][:])
+            result_m = keep.tile([P, P], F32, name=f"result1{m}")
+            copy(out=result_m[:], in_=acc_m[:])
+            queue.dma_start(out=out_view[:, m, target_halves[1]], in_=result_m[:])

from contextlib import ExitStack

import concourse.mybir as mybir
from concourse.masks import make_identity

K, T, S, D, V, H, N = 512, 1024, 512, 4, 256, 512, 256
FLOPS = 2 * K * H * S + 2 * H * N * V

F32 = mybir.dt.float32
BF16 = mybir.dt.bfloat16
U32 = mybir.dt.uint32
U16 = mybir.dt.uint16
U8 = mybir.dt.uint8
FP8X4 = mybir.dt.float8_e4m3fn_x4
MULT = mybir.AluOpType.mult
ADD = mybir.AluOpType.add
COPY = mybir.ActivationFunctionType.Copy

P = 128


def tile_picked_lapl_none_e_kernel(
    tc, xT, w1, w2, gate, offs, cen, pos1, pos2, pos3, pos4, out
):
    nc = tc.nc
    with ExitStack() as ctx:
        keep = ctx.enter_context(tc.tile_pool(name="keep", bufs=1))
        psum = ctx.enter_context(tc.psum_pool(name="psum", bufs=1))

        def bank(k, shape, name):
            return psum.tile(shape, F32, name=name, tag=f"bank{k}")

        def quantize(codes, scales, grouped):
            nc.vector.quantize_mx(out=codes.bitcast(FP8X4), scales=scales, in_=grouped)

        def product(acc, w_codes, w_scales, a_codes, a_scales):
            nc.tensor.matmul_mx(
                out=acc,
                lhsT=w_codes.bitcast(FP8X4),
                lhsT_scale=w_scales,
                rhs=a_codes.bitcast(FP8X4),
                rhs_scale=a_scales,
                start=True,
                stop=True,
            )

        offs_sb = keep.tile([P, S // 16], U16, name="offs_sb")
        nc.sync.dma_start(offs_sb[:], offs)
        x_rows = xT.rearrange("(p j) t -> p j t", j=4)
        x_plane = [keep.tile([P, T], F32, name=f"x_plane{j}") for j in range(4)]
        nc.sync.dma_start(out=x_plane[0][:], in_=x_rows[:, 0, :])
        gate_runs = keep.tile([P, 8], F32, name="gate_runs")
        nc.sync.dma_start(out=gate_runs[:], in_=gate.rearrange("d p (c i) -> (d p c) i", i=8)[0 : D * P * V // 8 : 129, :])
        for j in range(1, 4):
            nc.sync.dma_start(out=x_plane[j][:], in_=x_rows[:, j, :])
        w1_rows = w1.rearrange("(p j) c -> p j c", j=4)
        w1_half = [keep.tile([P, 4, H // 2], F32, name=f"w1_half{a}") for a in range(2)]
        for a in range(2):
            nc.sync.dma_start(out=w1_half[a][:], in_=w1_rows[:, :, a * 256 : (a + 1) * 256])
        lists = []
        for name, src in (("pos1", pos1), ("pos2", pos2), ("pos3", pos3), ("pos4", pos4), ("cen", cen)):
            list_sb = keep.tile([P, V // 16], U16, name=f"{name}_sb")
            nc.sync.dma_start(list_sb[:], src)
            lists.append(list_sb)
        cen_sb = lists[D]
        w2_raw = keep.tile([P, 4, N], F32, name="w2_raw")
        nc.sync.dma_start(out=w2_raw[:], in_=w2.rearrange("(p j) m -> p j m", j=4))

        ident = keep.tile([P, P], F32, name="ident")
        make_identity(nc, ident[:])

        neg_gate = keep.tile([P, D * V], F32, name="neg_gate")
        for c in range(2):
            spread = bank(c, [P, 4, P], "spread")
            for i in range(4):
                nc.tensor.transpose(
                    spread[:, i, :], gate_runs[:, 4 * c + i : 4 * c + i + 1].to_broadcast([P, P]), ident[:]
                )
            nc.scalar.activation(
                out=neg_gate[:].rearrange("p (q c i) -> p c q i", c=2, i=4)[:, c],
                in_=spread[:].rearrange("p i q -> p q i"),
                func=COPY,
                scale=-1.0,
            )

        node_halves = [slice(0, S // 2), slice(S // 2, S)]
        x_grouped = [keep.tile([P, 2 * S], BF16, name=f"x_grouped{b}", align_bytes=64) for b in range(2)]
        for u, weave in enumerate((nc.scalar.copy, nc.vector.tensor_copy)):
            picked = keep.tile([P, 2, S], F32, name=f"picked{u}")
            for e in range(2):
                nc.vector.tensor_copy(picked[:, e, :], x_plane[2 * u + e][:].indirect(offs_sb[:]))
            for b in range(2):
                weave(
                    out=x_grouped[b][:].rearrange("p (n u e) -> p u n e", u=2, e=2)[:, u],
                    in_=picked[:, :, node_halves[b]].rearrange("p e n -> p n e"),
                )

        w1_grouped = []
        for u in range(2):
            grouped = keep.tile([P, 2 * K], BF16, name=f"w1_grouped{u}", tag=f"w1_slot{u}", align_bytes=64)
            for a in range(2):
                nc.scalar.copy(
                    out=grouped[:].rearrange("p (e a m j) -> p a m j e", e=2, a=2, j=4)[:, a],
                    in_=w1_half[a][:].rearrange("p j (m u e) -> p u m j e", u=2, e=2)[:, u],
                )
            w1_grouped.append(grouped)

        w1_scales = keep.tile([P, H], U8, name="w1_scales", align_bytes=64)
        first_codes = keep.tile([P, P], U32, name="first_codes", tag="w1_codes", align_bytes=64)
        quantize(first_codes[:], w1_scales[:, 0:P], w1_grouped[0][:, 0:K])
        x_codes = keep.tile([P, S], U32, name="x_codes", align_bytes=64)
        x_scales = keep.tile([P, S], U8, name="x_scales", align_bytes=64)
        for b in range(2):
            quantize(x_codes[:, node_halves[b]], x_scales[:, node_halves[b]], x_grouped[b][:])

        h = [keep.tile([P, S], F32, name=f"h{t}") for t in range(4)]
        for b, copy in enumerate((nc.vector.tensor_copy, nc.scalar.copy)):
            cols = node_halves[b]
            acc = bank(4 + b, [P, S // 2], "h_acc")
            product(acc[:], first_codes[:], w1_scales[:, 0:P], x_codes[:, cols], x_scales[:, cols])
            copy(out=h[0][:, cols], in_=acc[:])

        later_codes = keep.tile([P, 3 * P], U32, name="later_codes", tag="w1_codes", align_bytes=64)
        quantize(later_codes[:, 0:P], w1_scales[:, P : 2 * P], w1_grouped[0][:, K : 2 * K])
        quantize(later_codes[:, P : 3 * P], w1_scales[:, 2 * P : 4 * P], w1_grouped[1][:])
        for t, k in ((1, 6), (2, 7), (3, 4)):
            acc = bank(k, [P, S], "h_acc")
            product(
                acc[:], later_codes[:, (t - 1) * P : t * P], w1_scales[:, t * P : (t + 1) * P], x_codes[:], x_scales[:]
            )
            nc.scalar.copy(out=h[t][:], in_=acc[:])

        target_halves = [slice(0, P), slice(P, V)]
        slots = {(0, 1): "w1_slot0", (0, 2): "w1_slot1", (0, 3): "w2_slot"}

        def neighbour_sum(t, back_banks):
            sums = [bank(2 * (t % 2) + b, [P, P], "turned_sum") for b in range(2)]
            for d in range(D):
                term = keep.tile([P, V], F32, name="term", tag=slots.get((t, d), f"term{t}{d}"), align_bytes=64)
                nc.vector.tensor_tensor(term[:], h[t][:].indirect(lists[d][:]), neg_gate[:, d * V : (d + 1) * V], MULT)
                for b in range(2):
                    nc.tensor.matmul(
                        sums[b][:],
                        lhsT=term[:, target_halves[b]],
                        rhs=ident[:],
                        is_transpose=True,
                        start=(d == 0),
                        stop=(d == D - 1),
                    )
            partial = keep.tile([P, V], F32, name=f"partial{t}")
            width = V // len(back_banks)
            back = [bank(k, [P, width], "back") for k in back_banks]
            for b in range(2):
                turned = keep.tile([P, P], F32, name="turned", tag=f"turned{t}{b}", align_bytes=64)
                nc.scalar.copy(out=turned[:], in_=sums[b][:])
                n, first = divmod(b * P, width)
                nc.tensor.transpose(back[n][:, first : first + P], turned[:], ident[:])
            for n in range(len(back_banks)):
                nc.scalar.copy(out=partial[:, n * width : (n + 1) * width], in_=back[n][:])
            return partial

        partials = [neighbour_sum(0, [5])]
        w2_grouped = keep.tile([P, N * 4], BF16, name="w2_grouped", tag="w2_slot", align_bytes=64)
        nc.scalar.copy(
            out=w2_grouped[:].rearrange("p (c i j) -> p c j i", i=4, j=4),
            in_=w2_raw[:].rearrange("p j (c i) -> p c j i", i=4),
        )
        partials.append(neighbour_sum(1, [6]))
        partials.append(neighbour_sum(2, [7]))
        partials.append(neighbour_sum(3, [4, 5]))

        w2_codes = keep.tile([P, N], U32, name="w2_codes", align_bytes=64)
        w2_scales = keep.tile([P, N], U8, name="w2_scales", align_bytes=64)
        quantize(w2_codes[:], w2_scales[:], w2_grouped[:])

        z_grouped = [
            keep.tile([P, 4 * P], BF16, name=f"z_grouped{b}", tag=f"turned3{b}", align_bytes=64) for b in range(2)
        ]
        z_slots = [g[:].rearrange("p (v u e) -> p u v e", u=2, e=2) for g in z_grouped]
        z01 = keep.tile([P, 2, V], F32, name="z01")
        for t in range(2):
            nc.vector.tensor_tensor(z01[:, t, :], h[t][:].indirect(cen_sb[:]), partials[t][:], ADD)
        for b in range(2):
            nc.scalar.copy(out=z_slots[b][:, 0], in_=z01[:, :, target_halves[b]].rearrange("p e v -> p v e"))
        z23 = [keep.tile([P, 2, P], F32, name=f"z23_{b}") for b in range(2)]
        for t in range(2, 4):
            for b in range(2):
                nc.vector.tensor_tensor(
                    z23[b][:, t - 2, :],
                    h[t][:].indirect(cen_sb[:, b * 8 : (b + 1) * 8]),
                    partials[t][:, target_halves[b]],
                    ADD,
                )
        for b in range(2):
            nc.vector.tensor_copy(out=z_slots[b][:, 1], in_=z23[b][:].rearrange("p e v -> p v e"))
        z_codes = [keep.tile([P, P], U32, name=f"z_codes{b}", align_bytes=64) for b in range(2)]
        z_scales = [keep.tile([P, P], U8, name=f"z_scales{b}", align_bytes=64) for b in range(2)]
        for b in range(2):
            quantize(z_codes[b][:], z_scales[b][:], z_grouped[b][:])

        out_view = out.rearrange("(m p) v -> p m v", p=P)
        acc = bank(0, [P, 2, P], "out_acc")
        for m in range(2):
            rows = slice(m * P, (m + 1) * P)
            product(acc[:, m, :], w2_codes[:, rows], w2_scales[:, rows], z_codes[0][:], z_scales[0][:])
        result = keep.tile([P, 2, P], F32, name="result0")
        nc.scalar.copy(out=result[:], in_=acc[:])
        nc.sync.dma_start(out=out_view[:, :, target_halves[0]], in_=result[:])
        for m, copy, queue in ((0, nc.vector.tensor_copy, nc.sync), (1, nc.scalar.copy, nc.scalar)):
            rows = slice(m * P, (m + 1) * P)
            acc_m = bank(1 + m, [P, P], "out_m")
            product(acc_m[:], w2_codes[:, rows], w2_scales[:, rows], z_codes[1][:], z_scales[1][:])
            result_m = keep.tile([P, P], F32, name=f"result1{m}")
            copy(out=result_m[:], in_=acc_m[:])
            queue.dma_start(out=out_view[:, m, target_halves[1]], in_=result_m[:])
